import numpy as np
import ml_dtypes


def mxq(x, axis, fmt="e4m3"):
    dtype, down = {"e4m3": (ml_dtypes.float8_e4m3fn, 7), "e5m2": (ml_dtypes.float8_e5m2, 14)}[fmt]
    v = np.moveaxis(np.asarray(x, np.float32).astype(ml_dtypes.bfloat16).astype(np.float64), axis, -1)
    blocks = v.reshape(v.shape[:-1] + (-1, 32))
    amax = np.abs(blocks).max(-1, keepdims=True)
    byte = np.maximum(np.where(amax > 0, np.frexp(amax)[1] - 1 + 127, 0) - down, 1)
    scale = np.exp2(byte - 127.0)
    codes = (blocks / scale).astype(np.float32).astype(dtype).astype(np.float64)
    return np.moveaxis((codes * scale).reshape(v.shape), -1, axis)


WIDE = False


def mx_kscale(k):
    if not WIDE:
        return np.ones(k)
    levels = np.array([10, -10, 5, -5, 0])
    if k % 512:
        return np.exp2(np.random.permutation(np.resize(levels, k // 32))).repeat(32)
    a = np.empty((k // 512, 16))
    for p in range(k // 512):
        a[p, :8] = np.random.permutation(np.resize(levels, 8))
        for g in range(8):
            far = levels[np.abs(levels - a[p, g]) >= 10]
            a[p, g + 8] = far[np.random.randint(len(far))]
    return np.exp2(a.ravel()).repeat(32)


def f64(x):
    return np.asarray(x).astype(np.float64)


def striped8(idx):
    return np.concatenate([v.reshape(-1, 16).T for v in idx]).astype(np.uint16)


def unstriped8(offs):
    return np.stack([offs[16 * g:16 * g + 16].T.reshape(-1) for g in range(8)]).astype(np.int64)


E2M1 = np.array([0.0, 0.5, 1.0, 1.5, 2.0, 3.0, 4.0, 6.0, -0.0, -0.5, -1.0, -1.5, -2.0, -3.0, -4.0, -6.0])


def pack_weight(w, fmt):
    k, n = w.shape
    w = f64(np.asarray(w, np.float32).astype(ml_dtypes.bfloat16)).reshape(k // 32, 32, n)
    amax = np.abs(w).max(1)
    if fmt == "e4m3":
        byte = np.frexp(amax)[1] - 1 + 127 - 7
    else:
        mant, ex = np.frexp(amax / 6.0)
        byte = np.where(mant > 0.5, ex, ex - 1) + 127
    byte = np.clip(np.where(amax > 0, byte, 1), 1, 254)
    scaled = (w * np.exp2(127.0 - byte)[:, None, :]).reshape(k, n).astype(np.float32)
    by_word = np.ascontiguousarray(scaled.reshape(k // 512, 128, 4, n).transpose(0, 1, 3, 2))
    if fmt == "e4m3":
        words = by_word.astype(ml_dtypes.float8_e4m3fn).view(np.uint8)
    else:
        c = by_word.astype(ml_dtypes.float4_e2m1fn).view(np.uint8) & 0xF
        words = (c[..., 0::2] | (c[..., 1::2] << 4)).reshape(k // 512, 128, 2 * n)
    return np.ascontiguousarray(words), np.ascontiguousarray(byte.astype(np.uint8).reshape(k // 512, 16, n))


def unpack_weight(words, scales, fmt):
    g, _, n = scales.shape
    words = np.ascontiguousarray(words).reshape(g, 128, n, -1)
    if fmt == "e4m3":
        vals = words.view(ml_dtypes.float8_e4m3fn).astype(np.float64)
    else:
        nib = np.empty((g, 128, n, 4), np.uint8)
        nib[..., 0::2] = words & 0xF
        nib[..., 1::2] = words >> 4
        vals = E2M1[nib]
    vals = vals * np.repeat(np.exp2(scales.astype(np.float64) - 127.0), 8, axis=1)[..., None]
    return vals.transpose(0, 1, 3, 2).reshape(g * 512, n)


K, M, T, S = 512, 512, 1024, 512


def setup_inputs():
    n = np.random.standard_normal
    s = mx_kscale(K)[:, None]
    u = mx_kscale(512)[:, None]
    p_w2 = pack_weight(1.4 * n((512, M)) / np.sqrt(512) / u, "e2m1")
    return {
        "x": (n((K, S)) * s).astype(np.float32),
        "w1": (n((K, 512)) / np.sqrt(K) / s * u.T).astype(np.float32),
        "w2_words": p_w2[0],
        "w2_scales": p_w2[1],
        "wgo": np.repeat(np.random.uniform(0.5, 2.0, (8, S)), 16, axis=0).astype(np.float32),
        "offs": striped8(np.stack([np.random.permutation(T)[:S] for _ in range(8)])),
    }


def reference(x, w1, w2_words, w2_scales, wgo, offs):
    x_ = mxq(f64(x), 0, "e4m3")
    w1_ = mxq(f64(w1), 0, "e4m3")
    w2_ = unpack_weight(w2_words, w2_scales, "e2m1")
    h_ = mxq(np.maximum(w1_.T @ x_, 0.0), 0, "e4m3")
    y = w2_.T @ h_
    place = unstriped8(offs)[np.arange(M) % 128 // 16]
    out = np.zeros((M, T))
    out[np.arange(M)[:, None], place] = f64(wgo)[np.arange(M) % 128] * (y)
    return out

@@ -1,0 +1,188 @@
+from contextlib import ExitStack
+
+import concourse.mybir as mybir
+
+K, H, M, T, S = 512, 512, 512, 1024, 512
+FLOPS = 2 * K * H * S + 2 * H * M * S
+
+F32 = mybir.dt.float32
+BF16 = mybir.dt.bfloat16
+I32 = mybir.dt.int32
+U32 = mybir.dt.uint32
+U16 = mybir.dt.uint16
+U8 = mybir.dt.uint8
+FP8X4 = mybir.dt.float8_e4m3fn_x4
+FP4X4 = mybir.dt.float4_e2m1fn_x4
+COPY = mybir.ActivationFunctionType.Copy
+RELU = mybir.ActivationFunctionType.Relu
+MULT = mybir.AluOpType.mult
+
+P = 128
+PACK = 4
+HALF = 64
+CHUNKS = ((0, 128), (128, 128), (256, 256))
+W1_PIECES = ((0, 64, 48), (64, 32, 8), (96, 32, 24))
+X0_VECTOR_SHARE = 0
+
+
+def tile_list_hscat_m_none_kernel(tc, x, w1, w2_words, w2_scales, wgo, offs, out):
+    nc = tc.nc
+    with ExitStack() as ctx:
+        sb = ctx.enter_context(tc.tile_pool(name="sb", bufs=1))
+        ps = ctx.enter_context(tc.psum_pool(name="ps", bufs=1))
+
+        offsets = sb.tile([P, S // 16], U16, name="offsets")
+        w2_plane = sb.tile([P, M], U8, name="w2_plane", align_bytes=64)
+        nc.vector.memset(w2_plane[:].bitcast(I32), 0)
+
+        w1_rows = w1.rearrange("(p j) r -> p j r", j=PACK)
+        x_rows = x.rearrange("(p j) c -> p j c", j=PACK)
+        w1_raw = [
+            sb.tile([P, PACK, PACK * count], F32, name=f"w1_raw{i}") for i, (m0, count, share) in enumerate(W1_PIECES)
+        ]
+        x_raw = [sb.tile([P, PACK, width], F32, name=f"x_raw{c}") for c, (j0, width) in enumerate(CHUNKS)]
+        w2_codes = sb.tile([P, 2 * M], U8, name="w2_codes", align_bytes=64)
+        weights = sb.tile([P, S], F32, name="weights")
+
+        def load_x(c):
+            j0, width = CHUNKS[c]
+            nc.sync.dma_start(out=x_raw[c][:], in_=x_rows[:, :, j0 : j0 + width])
+
+        def load_w1(i):
+            m0, count, share = W1_PIECES[i]
+            nc.sync.dma_start(out=w1_raw[i][:], in_=w1_rows[:, :, PACK * m0 : PACK * (m0 + count)])
+
+        load_x(0)
+        load_w1(0)
+        for q in range(4):
+            nc.sync.dma_start(
+                out=w2_plane[32 * q : 32 * q + 4, :].bitcast(I32),
+                in_=w2_scales[0, 4 * q : 4 * q + 4, :].bitcast(I32),
+            )
+        for i in range(1, len(W1_PIECES)):
+            load_w1(i)
+        load_x(1)
+        load_x(2)
+        nc.sync.dma_start(out=w2_codes[:].bitcast(I32), in_=w2_words[0].bitcast(I32))
+        nc.sync.dma_start(offsets[:], offs)
+        nc.sync.dma_start(out=weights[:], in_=wgo)
+
+        pages = [sb.tile([P, T], F32, name=f"page{t}") for t in range(PACK)]
+        for t in range(PACK):
+            (nc.vector if t < 2 else nc.gpsimd).memset(pages[t][:], 0.0)
+
+        def cast(dst, src, share):
+            count = dst.shape[1]
+            if share < count:
+                nc.scalar.activation(dst[:, share:count], src[:, share:count], COPY)
+            if share > 0:
+                nc.vector.tensor_copy(dst[:, 0:share], src[:, 0:share])
+
+        w1_codes = [sb.tile([P, P], U32, name=f"w1_codes{t}", align_bytes=64) for t in range(PACK)]
+        w1_plane = [sb.tile([P, P], U8, name=f"w1_plane{t}", align_bytes=64) for t in range(PACK)]
+        w1_bf = [sb.tile([P, PACK, HALF, PACK], BF16, name=f"w1_bf{h}", align_bytes=64) for h in range(2)]
+
+        def cast_w1(i):
+            m0, count, share = W1_PIECES[i]
+            h, m = divmod(m0, HALF)
+            cast(
+                w1_bf[h][:, :, m : m + count, :].rearrange("p t m j -> p m j t"),
+                w1_raw[i][:].rearrange("p j (m t) -> p m j t", t=PACK),
+                share,
+            )
+
+        def quantize_w1(h, t):
+            cols = slice(h * HALF, (h + 1) * HALF)
+            nc.vector.quantize_mx(
+                out=w1_codes[t][:, cols].bitcast(FP8X4),
+                scales=w1_plane[t][:, cols],
+                in_=w1_bf[h][:, t].rearrange("p m j -> p (m j)"),
+            )
+
+        def quantize(name, bf, tag=None):
+            width = bf.shape[1]
+            codes = sb.tile([P, width], U32, name=name + "_codes", tag=tag or name + "_codes", align_bytes=64)
+            plane = sb.tile([P, width], U8, name=name + "_plane", align_bytes=64)
+            nc.vector.quantize_mx(
+                out=codes[:].bitcast(FP8X4), scales=plane[:], in_=bf[:].rearrange("p c j -> p (c j)")
+            )
+            return codes, plane
+
+        def cast_x(c, share, tag):
+            width = CHUNKS[c][1]
+            bf = sb.tile([P, width, PACK], BF16, name=f"x_bf{c}", tag=tag, align_bytes=64)
+            cast(
+                bf[:].rearrange("p (c i) j -> p c j i", i=4),
+                x_raw[c][:].rearrange("p j (c i) -> p c j i", i=4),
+                share,
+            )
+            return bf
+
+        def hidden(c, xq, banks):
+            width = CHUNKS[c][1]
+            bf = sb.tile([P, width, PACK], BF16, name=f"h_bf{c}", tag=f"h_bf{c}", align_bytes=64)
+            for b, bank in enumerate(banks):
+                cols = slice(b * P, (b + 1) * P)
+                acc = ps.tile([P, PACK, P], F32, name=f"h_acc{c}_{b}", tag=bank)
+                for t in range(PACK):
+                    nc.tensor.matmul_mx(
+                        out=acc[:, t, :],
+                        lhsT=w1_codes[t][:].bitcast(FP8X4),
+                        lhsT_scale=w1_plane[t][:],
+                        rhs=xq[0][:, cols].bitcast(FP8X4),
+                        rhs_scale=xq[1][:, cols],
+                        start=True,
+                        stop=True,
+                    )
+                nc.scalar.activation(bf[:, cols, :], acc[:].rearrange("p t c -> p c t"), RELU)
+            return bf
+
+        def project(c, hq, tiles, bank):
+            width = CHUNKS[c][1]
+            acc = ps.tile([P, len(tiles), width], F32, name=f"y_acc{c}_{tiles[0]}", tag=bank)
+            for i, t in enumerate(tiles):
+                nc.tensor.matmul_mx(
+                    out=acc[:, i, :],
+                    lhsT=w2_codes[:, 2 * P * t : 2 * P * (t + 1)].bitcast(FP4X4),
+                    lhsT_scale=w2_plane[:, P * t : P * (t + 1)],
+                    rhs=hq[0][:].bitcast(FP8X4),
+                    rhs_scale=hq[1][:],
+                    start=True,
+                    stop=True,
+                )
+            y = sb.tile([P, len(tiles), width], F32, name=f"y{c}_{tiles[0]}")
+            nc.scalar.activation(y[:], acc[:], COPY)
+            return [y[:, i, :] for i in range(len(tiles))]
+
+        def scatter(c, t, y):
+            j0, width = CHUNKS[c]
+            nc.vector.tensor_tensor(
+                pages[t][:].indirect(offsets[:, j0 // 16 : (j0 + width) // 16]),
+                y,
+                weights[:, j0 : j0 + width],
+                MULT,
+            )
+
+        xq0 = quantize("x0", cast_x(0, X0_VECTOR_SHARE, "x_bf0"))
+        cast_w1(0)
+        for t in range(PACK):
+            quantize_w1(0, t)
+        for i in range(1, len(W1_PIECES)):
+            cast_w1(i)
+        for t in range(PACK):
+            quantize_w1(1, t)
+        h_bf0 = hidden(0, xq0, ["bank0"])
+        xq1 = quantize("x1", cast_x(1, 0, "x_bf1"))
+        x_bf2 = cast_x(2, 64, "x_bf2")
+        hq0 = quantize("h0", h_bf0)
+        y0 = project(0, hq0, [0], "bank4") + project(0, hq0, [1, 2, 3], "bank5")
+        xq2 = quantize("x2", x_bf2, "h_bf0")
+        hq1 = quantize("h1", hidden(1, xq1, ["bank1"]))
+        hq2 = quantize("h2", hidden(2, xq2, ["bank4", "bank5"]))
+        y1 = project(1, hq1, [0], "bank0") + project(1, hq1, [1, 2, 3], "bank5")
+        y2 = project(2, hq2, [0, 1], "bank6") + project(2, hq2, [2, 3], "bank7")
+        for c, y in enumerate((y0, y1, y2)):
+            for t in range(PACK):
+                scatter(c, t, y[t])
+                if c == len(CHUNKS) - 1:
+                    nc.sync.dma_start(out=out[t * P : (t + 1) * P, :], in_=pages[t][:])

@@ -21,7 +21,7 @@ P = 128
 PACK = 4
 HALF = 64
 CHUNKS = ((0, 128), (128, 128), (256, 256))
-W1_PIECES = ((0, 64, 48), (64, 32, 8), (96, 32, 24))
+W1_PIECES = ((0, 64, 48), (64, 32, 8), (96, 32, 16))
 X0_VECTOR_SHARE = 0
 
 
@@ -40,13 +40,12 @@ def tile_list_hscat_m_none_kernel(tc, x, w1, w2_words, w2_scales, wgo, offs, out
         w1_raw = [
             sb.tile([P, PACK, PACK * count], F32, name=f"w1_raw{i}") for i, (m0, count, share) in enumerate(W1_PIECES)
         ]
-        x_raw = [sb.tile([P, PACK, width], F32, name=f"x_raw{c}") for c, (j0, width) in enumerate(CHUNKS)]
+        x_raw = [sb.tile([P, PACK, P], F32, name=f"x_raw{i}") for i in range(S // P)]
         w2_codes = sb.tile([P, 2 * M], U8, name="w2_codes", align_bytes=64)
         weights = sb.tile([P, S], F32, name="weights")
 
         def load_x(c):
-            j0, width = CHUNKS[c]
-            nc.sync.dma_start(out=x_raw[c][:], in_=x_rows[:, :, j0 : j0 + width])
+            nc.sync.dma_start(out=x_raw[c][:], in_=x_rows[:, :, c * P : (c + 1) * P])
 
         def load_w1(i):
             m0, count, share = W1_PIECES[i]
@@ -63,13 +62,14 @@ def tile_list_hscat_m_none_kernel(tc, x, w1, w2_words, w2_scales, wgo, offs, out
             load_w1(i)
         load_x(1)
         load_x(2)
+        load_x(3)
         nc.sync.dma_start(out=w2_codes[:].bitcast(I32), in_=w2_words[0].bitcast(I32))
         nc.sync.dma_start(offsets[:], offs)
         nc.sync.dma_start(out=weights[:], in_=wgo)
 
         pages = [sb.tile([P, T], F32, name=f"page{t}") for t in range(PACK)]
         for t in range(PACK):
-            (nc.vector if t < 2 else nc.gpsimd).memset(pages[t][:], 0.0)
+            nc.vector.memset(pages[t][:], 0.0)
 
         def cast(dst, src, share):
             count = dst.shape[1]
@@ -108,14 +108,15 @@ def tile_list_hscat_m_none_kernel(tc, x, w1, w2_words, w2_scales, wgo, offs, out
             )
             return codes, plane
 
-        def cast_x(c, share, tag):
-            width = CHUNKS[c][1]
-            bf = sb.tile([P, width, PACK], BF16, name=f"x_bf{c}", tag=tag, align_bytes=64)
-            cast(
-                bf[:].rearrange("p (c i) j -> p c j i", i=4),
-                x_raw[c][:].rearrange("p j (c i) -> p c j i", i=4),
-                share,
-            )
+        def cast_x(c, share):
+            j0, width = CHUNKS[c]
+            bf = sb.tile([P, width, PACK], BF16, name=f"x_bf{c}", align_bytes=64)
+            for b in range(width // P):
+                cast(
+                    bf[:, b * P : (b + 1) * P, :].rearrange("p (c i) j -> p c j i", i=4),
+                    x_raw[j0 // P + b][:].rearrange("p j (c i) -> p c j i", i=4),
+                    share,
+                )
             return bf
 
         def hidden(c, xq, banks):
@@ -137,33 +138,36 @@ def tile_list_hscat_m_none_kernel(tc, x, w1, w2_words, w2_scales, wgo, offs, out
                 nc.scalar.activation(bf[:, cols, :], acc[:].rearrange("p t c -> p c t"), RELU)
             return bf
 
-        def project(c, hq, tiles, bank):
-            width = CHUNKS[c][1]
-            acc = ps.tile([P, len(tiles), width], F32, name=f"y_acc{c}_{tiles[0]}", tag=bank)
+        def project(parts, tiles, bank):
+            width = sum(hq[0].shape[1] for hq in parts)
+            name = f"{bank}_{width}_{tiles[0]}"
+            acc = ps.tile([P, len(tiles), width], F32, name="y_acc" + name, tag=bank)
             for i, t in enumerate(tiles):
-                nc.tensor.matmul_mx(
-                    out=acc[:, i, :],
-                    lhsT=w2_codes[:, 2 * P * t : 2 * P * (t + 1)].bitcast(FP4X4),
-                    lhsT_scale=w2_plane[:, P * t : P * (t + 1)],
-                    rhs=hq[0][:].bitcast(FP8X4),
-                    rhs_scale=hq[1][:],
-                    start=True,
-                    stop=True,
-                )
-            y = sb.tile([P, len(tiles), width], F32, name=f"y{c}_{tiles[0]}")
+                col = 0
+                for codes, plane in parts:
+                    nc.tensor.matmul_mx(
+                        out=acc[:, i, col : col + codes.shape[1]],
+                        lhsT=w2_codes[:, 2 * P * t : 2 * P * (t + 1)].bitcast(FP4X4),
+                        lhsT_scale=w2_plane[:, P * t : P * (t + 1)],
+                        rhs=codes[:].bitcast(FP8X4),
+                        rhs_scale=plane[:],
+                        start=True,
+                        stop=True,
+                    )
+                    col = col + codes.shape[1]
+            y = sb.tile([P, len(tiles), width], F32, name="y" + name)
             nc.scalar.activation(y[:], acc[:], COPY)
             return [y[:, i, :] for i in range(len(tiles))]
 
-        def scatter(c, t, y):
-            j0, width = CHUNKS[c]
+        def scatter(j0, t, y):
+            j1 = j0 + y.shape[1]
             nc.vector.tensor_tensor(
-                pages[t][:].indirect(offsets[:, j0 // 16 : (j0 + width) // 16]),
-                y,
-                weights[:, j0 : j0 + width],
-                MULT,
+                pages[t][:].indirect(offsets[:, j0 // 16 : j1 // 16]), y, weights[:, j0:j1], MULT
             )
+            if j1 == S:
+                nc.sync.dma_start(out=out[t * P : (t + 1) * P, :], in_=pages[t][:])
 
-        xq0 = quantize("x0", cast_x(0, X0_VECTOR_SHARE, "x_bf0"))
+        xq0 = quantize("x0", cast_x(0, X0_VECTOR_SHARE))
         cast_w1(0)
         for t in range(PACK):
             quantize_w1(0, t)
@@ -172,17 +176,21 @@ def tile_list_hscat_m_none_kernel(tc, x, w1, w2_words, w2_scales, wgo, offs, out
         for t in range(PACK):
             quantize_w1(1, t)
         h_bf0 = hidden(0, xq0, ["bank0"])
-        xq1 = quantize("x1", cast_x(1, 0, "x_bf1"))
-        x_bf2 = cast_x(2, 64, "x_bf2")
+        xq1 = quantize("x1", cast_x(1, 0))
+        x_bf2 = cast_x(2, 32)
         hq0 = quantize("h0", h_bf0)
-        y0 = project(0, hq0, [0], "bank4") + project(0, hq0, [1, 2, 3], "bank5")
+        y0 = project([hq0], [0], "bank4") + project([hq0], [1, 2, 3], "bank5")
         xq2 = quantize("x2", x_bf2, "h_bf0")
         hq1 = quantize("h1", hidden(1, xq1, ["bank1"]))
         hq2 = quantize("h2", hidden(2, xq2, ["bank4", "bank5"]))
-        y1 = project(1, hq1, [0], "bank0") + project(1, hq1, [1, 2, 3], "bank5")
-        y2 = project(2, hq2, [0, 1], "bank6") + project(2, hq2, [2, 3], "bank7")
-        for c, y in enumerate((y0, y1, y2)):
-            for t in range(PACK):
-                scatter(c, t, y[t])
-                if c == len(CHUNKS) - 1:
-                    nc.sync.dma_start(out=out[t * P : (t + 1) * P, :], in_=pages[t][:])
+        y1 = project([hq1], [0, 1], "bank5")
+        y12 = project([hq1, hq2], [2], "bank2") + project([hq1, hq2], [3], "bank3")
+        y2 = project([hq2], [0, 1], "bank6")
+        for t in range(4):
+            scatter(0, t, y0[t])
+        for t in range(2):
+            scatter(128, t, y1[t])
+        for t in range(2):
+            scatter(128, 2 + t, y12[t])
+        for t in range(2):
+            scatter(256, t, y2[t])

from contextlib import ExitStack

import concourse.mybir as mybir

K, H, M, T, S = 512, 512, 512, 1024, 512
FLOPS = 2 * K * H * S + 2 * H * M * S

F32 = mybir.dt.float32
BF16 = mybir.dt.bfloat16
I32 = mybir.dt.int32
U32 = mybir.dt.uint32
U16 = mybir.dt.uint16
U8 = mybir.dt.uint8
FP8X4 = mybir.dt.float8_e4m3fn_x4
FP4X4 = mybir.dt.float4_e2m1fn_x4
COPY = mybir.ActivationFunctionType.Copy
RELU = mybir.ActivationFunctionType.Relu
MULT = mybir.AluOpType.mult

P = 128
PACK = 4
HALF = 64
CHUNKS = ((0, 128), (128, 128), (256, 256))
W1_PIECES = ((0, 64, 48), (64, 32, 8), (96, 32, 16))
X0_VECTOR_SHARE = 0


def tile_list_hscat_m_none_kernel(tc, x, w1, w2_words, w2_scales, wgo, offs, out):
    nc = tc.nc
    with ExitStack() as ctx:
        sb = ctx.enter_context(tc.tile_pool(name="sb", bufs=1))
        ps = ctx.enter_context(tc.psum_pool(name="ps", bufs=1))

        offsets = sb.tile([P, S // 16], U16, name="offsets")
        w2_plane = sb.tile([P, M], U8, name="w2_plane", align_bytes=64)
        nc.vector.memset(w2_plane[:].bitcast(I32), 0)

        w1_rows = w1.rearrange("(p j) r -> p j r", j=PACK)
        x_rows = x.rearrange("(p j) c -> p j c", j=PACK)
        w1_raw = [
            sb.tile([P, PACK, PACK * count], F32, name=f"w1_raw{i}") for i, (m0, count, share) in enumerate(W1_PIECES)
        ]
        x_raw = [sb.tile([P, PACK, P], F32, name=f"x_raw{i}") for i in range(S // P)]
        w2_codes = sb.tile([P, 2 * M], U8, name="w2_codes", align_bytes=64)
        weights = sb.tile([P, S], F32, name="weights")

        def load_x(c):
            nc.sync.dma_start(out=x_raw[c][:], in_=x_rows[:, :, c * P : (c + 1) * P])

        def load_w1(i):
            m0, count, share = W1_PIECES[i]
            nc.sync.dma_start(out=w1_raw[i][:], in_=w1_rows[:, :, PACK * m0 : PACK * (m0 + count)])

        load_x(0)
        load_w1(0)
        for q in range(4):
            nc.sync.dma_start(
                out=w2_plane[32 * q : 32 * q + 4, :].bitcast(I32),
                in_=w2_scales[0, 4 * q : 4 * q + 4, :].bitcast(I32),
            )
        for i in range(1, len(W1_PIECES)):
            load_w1(i)
        load_x(1)
        load_x(2)
        load_x(3)
        nc.sync.dma_start(out=w2_codes[:].bitcast(I32), in_=w2_words[0].bitcast(I32))
        nc.sync.dma_start(offsets[:], offs)
        nc.sync.dma_start(out=weights[:], in_=wgo)

        pages = [sb.tile([P, T], F32, name=f"page{t}") for t in range(PACK)]
        for t in range(PACK):
            nc.vector.memset(pages[t][:], 0.0)

        def cast(dst, src, share):
            count = dst.shape[1]
            if share < count:
                nc.scalar.activation(dst[:, share:count], src[:, share:count], COPY)
            if share > 0:
                nc.vector.tensor_copy(dst[:, 0:share], src[:, 0:share])

        w1_codes = [sb.tile([P, P], U32, name=f"w1_codes{t}", align_bytes=64) for t in range(PACK)]
        w1_plane = [sb.tile([P, P], U8, name=f"w1_plane{t}", align_bytes=64) for t in range(PACK)]
        w1_bf = [sb.tile([P, PACK, HALF, PACK], BF16, name=f"w1_bf{h}", align_bytes=64) for h in range(2)]

        def cast_w1(i):
            m0, count, share = W1_PIECES[i]
            h, m = divmod(m0, HALF)
            cast(
                w1_bf[h][:, :, m : m + count, :].rearrange("p t m j -> p m j t"),
                w1_raw[i][:].rearrange("p j (m t) -> p m j t", t=PACK),
                share,
            )

        def quantize_w1(h, t):
            cols = slice(h * HALF, (h + 1) * HALF)
            nc.vector.quantize_mx(
                out=w1_codes[t][:, cols].bitcast(FP8X4),
                scales=w1_plane[t][:, cols],
                in_=w1_bf[h][:, t].rearrange("p m j -> p (m j)"),
            )

        def quantize(name, bf, tag=None):
            width = bf.shape[1]
            codes = sb.tile([P, width], U32, name=name + "_codes", tag=tag or name + "_codes", align_bytes=64)
            plane = sb.tile([P, width], U8, name=name + "_plane", align_bytes=64)
            nc.vector.quantize_mx(
                out=codes[:].bitcast(FP8X4), scales=plane[:], in_=bf[:].rearrange("p c j -> p (c j)")
            )
            return codes, plane

        def cast_x(c, share):
            j0, width = CHUNKS[c]
            bf = sb.tile([P, width, PACK], BF16, name=f"x_bf{c}", align_bytes=64)
            for b in range(width // P):
                cast(
                    bf[:, b * P : (b + 1) * P, :].rearrange("p (c i) j -> p c j i", i=4),
                    x_raw[j0 // P + b][:].rearrange("p j (c i) -> p c j i", i=4),
                    share,
                )
            return bf

        def hidden(c, xq, banks):
            width = CHUNKS[c][1]
            bf = sb.tile([P, width, PACK], BF16, name=f"h_bf{c}", tag=f"h_bf{c}", align_bytes=64)
            for b, bank in enumerate(banks):
                cols = slice(b * P, (b + 1) * P)
                acc = ps.tile([P, PACK, P], F32, name=f"h_acc{c}_{b}", tag=bank)
                for t in range(PACK):
                    nc.tensor.matmul_mx(
                        out=acc[:, t, :],
                        lhsT=w1_codes[t][:].bitcast(FP8X4),
                        lhsT_scale=w1_plane[t][:],
                        rhs=xq[0][:, cols].bitcast(FP8X4),
                        rhs_scale=xq[1][:, cols],
                        start=True,
                        stop=True,
                    )
                nc.scalar.activation(bf[:, cols, :], acc[:].rearrange("p t c -> p c t"), RELU)
            return bf

        def project(parts, tiles, bank):
            width = sum(hq[0].shape[1] for hq in parts)
            name = f"{bank}_{width}_{tiles[0]}"
            acc = ps.tile([P, len(tiles), width], F32, name="y_acc" + name, tag=bank)
            for i, t in enumerate(tiles):
                col = 0
                for codes, plane in parts:
                    nc.tensor.matmul_mx(
                        out=acc[:, i, col : col + codes.shape[1]],
                        lhsT=w2_codes[:, 2 * P * t : 2 * P * (t + 1)].bitcast(FP4X4),
                        lhsT_scale=w2_plane[:, P * t : P * (t + 1)],
                        rhs=codes[:].bitcast(FP8X4),
                        rhs_scale=plane[:],
                        start=True,
                        stop=True,
                    )
                    col = col + codes.shape[1]
            y = sb.tile([P, len(tiles), width], F32, name="y" + name)
            nc.scalar.activation(y[:], acc[:], COPY)
            return [y[:, i, :] for i in range(len(tiles))]

        def scatter(j0, t, y):
            j1 = j0 + y.shape[1]
            nc.vector.tensor_tensor(
                pages[t][:].indirect(offsets[:, j0 // 16 : j1 // 16]), y, weights[:, j0:j1], MULT
            )
            if j1 == S:
                nc.sync.dma_start(out=out[t * P : (t + 1) * P, :], in_=pages[t][:])

        xq0 = quantize("x0", cast_x(0, X0_VECTOR_SHARE))
        cast_w1(0)
        for t in range(PACK):
            quantize_w1(0, t)
        for i in range(1, len(W1_PIECES)):
            cast_w1(i)
        for t in range(PACK):
            quantize_w1(1, t)
        h_bf0 = hidden(0, xq0, ["bank0"])
        xq1 = quantize("x1", cast_x(1, 0))
        x_bf2 = cast_x(2, 32)
        hq0 = quantize("h0", h_bf0)
        y0 = project([hq0], [0], "bank4") + project([hq0], [1, 2, 3], "bank5")
        xq2 = quantize("x2", x_bf2, "h_bf0")
        hq1 = quantize("h1", hidden(1, xq1, ["bank1"]))
        hq2 = quantize("h2", hidden(2, xq2, ["bank4", "bank5"]))
        y1 = project([hq1], [0, 1], "bank5")
        y12 = project([hq1, hq2], [2], "bank2") + project([hq1, hq2], [3], "bank3")
        y2 = project([hq2], [0, 1], "bank6")
        for t in range(4):
            scatter(0, t, y0[t])
        for t in range(2):
            scatter(128, t, y1[t])
        for t in range(2):
            scatter(128, 2 + t, y12[t])
        for t in range(2):
            scatter(256, t, y2[t])
